import numpy as np
import ml_dtypes


def mxq(x, axis, fmt="e4m3"):
    dtype, down = {"e4m3": (ml_dtypes.float8_e4m3fn, 7), "e5m2": (ml_dtypes.float8_e5m2, 14)}[fmt]
    v = np.moveaxis(np.asarray(x, np.float32).astype(ml_dtypes.bfloat16).astype(np.float64), axis, -1)
    blocks = v.reshape(v.shape[:-1] + (-1, 32))
    amax = np.abs(blocks).max(-1, keepdims=True)
    byte = np.maximum(np.where(amax > 0, np.frexp(amax)[1] - 1 + 127, 0) - down, 1)
    scale = np.exp2(byte - 127.0)
    codes = (blocks / scale).astype(np.float32).astype(dtype).astype(np.float64)
    return np.moveaxis((codes * scale).reshape(v.shape), -1, axis)


WIDE = False


def mx_kscale(k):
    if not WIDE:
        return np.ones(k)
    levels = np.array([30, -30])
    if k % 512:
        return np.exp2(np.random.permutation(np.resize(levels, k // 32))).repeat(32)
    a = np.empty((k // 512, 16))
    for p in range(k // 512):
        a[p, :8] = np.random.permutation(np.resize(levels, 8))
        for g in range(8):
            far = levels[np.abs(levels - a[p, g]) >= 10]
            a[p, g + 8] = far[np.random.randint(len(far))]
    return np.exp2(a.ravel()).repeat(32)


def f64(x):
    return np.asarray(x).astype(np.float64)


def striped(idx):
    return np.tile(np.asarray(idx).reshape(-1, 16).T, (8, 1)).astype(np.uint16)


def unstriped(offs):
    return offs[:16].T.reshape(-1).astype(np.int64)


E2M1 = np.array([0.0, 0.5, 1.0, 1.5, 2.0, 3.0, 4.0, 6.0, -0.0, -0.5, -1.0, -1.5, -2.0, -3.0, -4.0, -6.0])


def pack_weight(w, fmt):
    k, n = w.shape
    w = f64(np.asarray(w, np.float32).astype(ml_dtypes.bfloat16)).reshape(k // 32, 32, n)
    amax = np.abs(w).max(1)
    if fmt in ("e4m3", "e5m2"):
        byte = np.frexp(amax)[1] - 1 + 127 - (7 if fmt == "e4m3" else 14)
    else:
        mant, ex = np.frexp(amax / 6.0)
        byte = np.where(mant > 0.5, ex, ex - 1) + 127
    byte = np.clip(np.where(amax > 0, byte, 1), 1, 254)
    scaled = (w * np.exp2(127.0 - byte)[:, None, :]).reshape(k, n).astype(np.float32)
    by_word = np.ascontiguousarray(scaled.reshape(k // 512, 128, 4, n).transpose(0, 1, 3, 2))
    if fmt in ("e4m3", "e5m2"):
        words = by_word.astype(ml_dtypes.float8_e4m3fn if fmt == "e4m3" else ml_dtypes.float8_e5m2).view(np.uint8)
    else:
        c = by_word.astype(ml_dtypes.float4_e2m1fn).view(np.uint8) & 0xF
        words = (c[..., 0::2] | (c[..., 1::2] << 4)).reshape(k // 512, 128, 2 * n)
    return np.ascontiguousarray(words), np.ascontiguousarray(byte.astype(np.uint8).reshape(k // 512, 16, n))


def unpack_weight(words, scales, fmt):
    g, _, n = scales.shape
    words = np.ascontiguousarray(words).reshape(g, 128, n, -1)
    if fmt in ("e4m3", "e5m2"):
        vals = words.view(ml_dtypes.float8_e4m3fn if fmt == "e4m3" else ml_dtypes.float8_e5m2).astype(np.float64)
    else:
        nib = np.empty((g, 128, n, 4), np.uint8)
        nib[..., 0::2] = words & 0xF
        nib[..., 1::2] = words >> 4
        vals = E2M1[nib]
    vals = vals * np.repeat(np.exp2(scales.astype(np.float64) - 127.0), 8, axis=1)[..., None]
    return vals.transpose(0, 1, 3, 2).reshape(g * 512, n)


def sigmoid(v):
    return 1.0 / (1.0 + np.exp(-v))


K, F, T, Z, J, R, C, Q, O, N, E = 512, 512, 1024, 1024, 256, 512, 512, 1024, 256, 256, 1024


def setup_inputs():
    n = np.random.standard_normal
    idx = np.random.permutation(T)[:J]
    idx2 = np.random.permutation(Z)[:J]
    idx3 = np.random.permutation(C)[:J]
    idx4 = np.random.permutation(Q)[:C]
    idx5 = np.random.permutation(C)[:O]
    idx6 = np.random.permutation(E)[:O]
    fk = mx_kscale(K)
    fr = mx_kscale(R)
    ff = mx_kscale(F)
    xtp = pack_weight(n((K, T)) / fk[:, None], "e4m3")
    wp = pack_weight(n((K, R)) * 1 / np.sqrt(K) * fk[:, None] * fr, "e2m1")
    xop = pack_weight(n((F, Z)) / ff[:, None], "e2m1")
    w0p = pack_weight(n((F, R)) * 1 / np.sqrt(F) * ff[:, None] * fr, "e5m2")
    wbp = pack_weight(n((R, N)) * 1 / np.sqrt(R) / fr[:, None], "e5m2")
    return {
        "xt_words": xtp[0],
        "xt_scales": xtp[1],
        "w_words": wp[0],
        "w_scales": wp[1],
        "xo_words": xop[0],
        "xo_scales": xop[1],
        "w0_words": w0p[0],
        "w0_scales": w0p[1],
        "tg": (1.0 * n((R, Q))).astype(np.float32),
        "sg": (np.random.uniform(0.6, 1.6, (R, 1))).astype(np.float32),
        "bg": (np.random.uniform(-1.0, 1.0, (R, 1))).astype(np.float32),
        "wb_words": wbp[0],
        "wb_scales": wbp[1],
        "offs": striped(idx),
        "offs2": striped(idx2),
        "offs3": striped(idx3),
        "offs4": striped(idx4),
        "offs5": striped(idx5),
        "offs6": striped(idx6),
    }


def reference(xt_words, xt_scales, w_words, w_scales, xo_words, xo_scales, w0_words, w0_scales, tg, sg, bg, wb_words, wb_scales, offs, offs2, offs3, offs4, offs5, offs6):
    idx = unstriped(offs)
    idx2 = unstriped(offs2)
    idx3 = unstriped(offs3)
    idx4 = unstriped(offs4)
    idx5 = unstriped(offs5)
    idx6 = unstriped(offs6)
    xtu = unpack_weight(xt_words, xt_scales, "e4m3")
    wu = unpack_weight(w_words, w_scales, "e2m1")
    xou = unpack_weight(xo_words, xo_scales, "e2m1")
    w0u = unpack_weight(w0_words, w0_scales, "e5m2")
    wbu = unpack_weight(wb_words, wb_scales, "e5m2")
    xtidxg = xtu[:, idx]
    xoidx2g = xou[:, idx2]
    a = wu.T @ xtidxg + w0u.T @ xoidx2g
    pw = np.zeros((R, C))
    pw[:, idx3] = a
    pg = pw * sigmoid(f64(tg)[:, idx4] * f64(sg) + f64(bg))
    hid = pg[:, idx5]
    hidq = mxq(hid, 0, "e4m3")
    p = wbu.T @ hidq
    y = np.zeros((N, E))
    y[:, idx6] = p
    return y

@@ -1,0 +1,186 @@
+from contextlib import ExitStack
+
+import concourse.mybir as mybir
+
+F32 = mybir.dt.float32
+BF16 = mybir.dt.bfloat16
+I32 = mybir.dt.int32
+U32 = mybir.dt.uint32
+U16 = mybir.dt.uint16
+U8 = mybir.dt.uint8
+E4M3X4 = mybir.dt.float8_e4m3fn_x4
+E5M2X4 = mybir.dt.float8_e5m2_x4
+E2M1X4 = mybir.dt.float4_e2m1fn_x4
+ACT = mybir.ActivationFunctionType
+MULT = mybir.AluOpType.mult
+
+P = 128
+PACK = 4
+T, Z, J, R, C, Q, O, N, E = 1024, 1024, 256, 512, 512, 1024, 256, 256, 1024
+FLOPS = 2 * 512 * R * J * 2 + 2 * R * N * O
+
+
+def load_scale_rows(queue, plane, scales):
+    for quad in range(4):
+        queue.dma_start(
+            out=plane[32 * quad : 32 * quad + 4, :].bitcast(I32),
+            in_=scales[0, 4 * quad : 4 * quad + 4, :].bitcast(I32),
+        )
+
+
+def deal_columns(nc, dealt, natural, run):
+    nc.vector.tensor_copy(
+        out=dealt.rearrange("p (t c i) -> p c t i", t=PACK, i=run),
+        in_=natural.rearrange("p (c i t) -> p c t i", t=PACK, i=run),
+    )
+
+
+def tile_list_gatedpage_bank_one_scattered_kernel(
+    tc, xt_words, xt_scales, w_words, w_scales, xo_words, xo_scales, w0_words, w0_scales,
+    tg, sg, bg, wb_words, wb_scales, offs, offs2, offs3, offs4, offs5, offs6, out,
+):
+    nc = tc.nc
+    with ExitStack() as ctx:
+        lists = ctx.enter_context(tc.tile_pool(name="lists", bufs=1))
+        sb = ctx.enter_context(tc.tile_pool(name="sb", bufs=1))
+        psum = ctx.enter_context(tc.psum_pool(name="psum", bufs=1))
+
+        idx = lists.tile([P, J // 16], U16, name="idx")
+        idx2 = lists.tile([P, J // 16], U16, name="idx2")
+        idx3 = lists.tile([P, J // 16], U16, name="idx3")
+        idx4 = lists.tile([P, C // 16], U16, name="idx4")
+        idx5 = lists.tile([P, O // 16], U16, name="idx5")
+        idx6 = lists.tile([P, O // 16], U16, name="idx6")
+
+        xt_w = sb.tile([P, T], U32, name="xt_w", align_bytes=64)
+        xt_s = sb.tile([P, T], U8, name="xt_s", align_bytes=64)
+        xo_w = sb.tile([P, Z], U16, name="xo_w", align_bytes=64)
+        xo_s = sb.tile([P, Z], U8, name="xo_s", align_bytes=64)
+        w_w = sb.tile([P, R], U16, name="w_w", align_bytes=64)
+        w0_w = sb.tile([P, R], I32, name="w0_w", align_bytes=64)
+        wb_w = sb.tile([P, N], I32, name="wb_w", align_bytes=64)
+        weight_s = sb.tile([P, R + R + N], U8, name="weight_s", align_bytes=64)
+        w_s, w0_s, wb_s = weight_s[:, 0:R], weight_s[:, R : 2 * R], weight_s[:, 2 * R :]
+        slope = sb.tile([P, PACK], F32, name="slope")
+        offset = sb.tile([P, PACK], F32, name="offset")
+        gates = [sb.tile([P, Q], F32, name="gates%d" % t) for t in range(PACK)]
+        board = [sb.tile([P, C], F32, name="board%d" % t) for t in range(PACK)]
+        page = [sb.tile([P, E], F32, name="page%d" % h) for h in range(N // P)]
+
+        nc.vector.memset(xt_s[:].bitcast(I32), 0)
+        nc.vector.memset(xo_s[:].bitcast(I32), 0)
+        nc.vector.memset(weight_s[:].bitcast(I32), 0)
+        for t in range(PACK):
+            nc.vector.memset(board[t][:], 0.0)
+
+        tg_rows = tg.rearrange("(p t) q -> p t q", t=PACK)
+        nc.sync.dma_start(idx[:], offs)
+        nc.sync.dma_start(idx2[:], offs2)
+        nc.sync.dma_start(out=xt_w[:].bitcast(I32), in_=xt_words[0].rearrange("p n t -> p (n t)").bitcast(I32))
+        load_scale_rows(nc.scalar, xt_s, xt_scales)
+        nc.sync.dma_start(out=xo_w[:].bitcast(I32), in_=xo_words[0].bitcast(I32))
+        load_scale_rows(nc.scalar, xo_s, xo_scales)
+        nc.sync.dma_start(out=w_w[:].bitcast(I32), in_=w_words[0].bitcast(I32))
+        nc.sync.dma_start(out=w0_w[:], in_=w0_words[0].rearrange("p n t -> p (n t)").bitcast(I32))
+        load_scale_rows(nc.sync, w_s, w_scales)
+        load_scale_rows(nc.sync, w0_s, w0_scales)
+        nc.sync.dma_start(out=gates[0][:], in_=tg_rows[:, 0, :])
+        nc.sync.dma_start(idx4[:], offs4)
+        nc.sync.dma_start(out=slope[:], in_=sg.rearrange("(p t) o -> p (t o)", t=PACK))
+        nc.sync.dma_start(out=offset[:], in_=bg.rearrange("(p t) o -> p (t o)", t=PACK))
+        nc.sync.dma_start(out=gates[1][:], in_=tg_rows[:, 1, :])
+        nc.sync.dma_start(idx3[:], offs3)
+        nc.sync.dma_start(out=gates[2][:], in_=tg_rows[:, 2, :])
+        nc.sync.dma_start(out=gates[3][:], in_=tg_rows[:, 3, :])
+        nc.sync.dma_start(idx5[:], offs5)
+        nc.sync.dma_start(idx6[:], offs6)
+        nc.sync.dma_start(out=wb_w[:], in_=wb_words[0].rearrange("p n t -> p (n t)").bitcast(I32))
+        load_scale_rows(nc.sync, wb_s, wb_scales)
+        for h in range(N // P):
+            nc.vector.memset(page[h][:], 0.0)
+
+        tok_w = sb.tile([P, J], U32, name="tok_w", align_bytes=64)
+        tok_s = sb.tile([P, J], U8, name="tok_s", align_bytes=64)
+        note_w = sb.tile([P, J], U16, name="note_w", align_bytes=64)
+        note_s = sb.tile([P, J], U8, name="note_s", align_bytes=64)
+        w_wd = sb.tile([P, R], U16, name="w_wd", align_bytes=64)
+        w0_wd = sb.tile([P, R], I32, name="w0_wd", align_bytes=64)
+        w_sd = sb.tile([P, R], U8, name="w_sd", align_bytes=64)
+        w0_sd = sb.tile([P, R], U8, name="w0_sd", align_bytes=64)
+        nc.vector.tensor_copy(tok_w[:], xt_w[:].indirect(idx[:]))
+        nc.vector.tensor_copy(note_w[:], xo_w[:].indirect(idx2[:]))
+        nc.vector.tensor_copy(tok_s[:], xt_s[:].indirect(idx[:]))
+        deal_columns(nc, w_wd[:], w_w[:], 8)
+        deal_columns(nc, w0_wd[:], w0_w[:], 4)
+        nc.vector.tensor_copy(note_s[:], xo_s[:].indirect(idx2[:]))
+        deal_columns(nc, w_sd[:], w_s, 16)
+        deal_columns(nc, w0_sd[:], w0_s, 16)
+
+        gate = [sb.tile([P, C], F32, name="gate%d" % t) for t in range(PACK)]
+        for t in range(PACK):
+            nc.scalar.activation(
+                out=gate[t][:], in_=gates[t][:].indirect(idx4[:]), func=ACT.Sigmoid,
+                bias=offset[:, t : t + 1], scale=slope[:, t : t + 1],
+            )
+
+        a_ps = [psum.tile([P, J], F32, name="a_ps%d" % t) for t in range(PACK)]
+        for t in (0, 2, 1, 3):
+            cols = slice(P * t, P * (t + 1))
+            nc.tensor.matmul_mx(
+                out=a_ps[t][:], lhsT=w_wd[:, cols].bitcast(E2M1X4), lhsT_scale=w_sd[:, cols],
+                rhs=tok_w[:].bitcast(E4M3X4), rhs_scale=tok_s[:], start=True, stop=False,
+            )
+            nc.tensor.matmul_mx(
+                out=a_ps[t][:], lhsT=w0_wd[:, cols].bitcast(E5M2X4), lhsT_scale=w0_sd[:, cols],
+                rhs=note_w[:].bitcast(E2M1X4), rhs_scale=note_s[:], start=False, stop=True,
+            )
+
+        a_sb = [sb.tile([P, J], F32, name="a_sb%d" % t) for t in range(PACK)]
+        gated = [sb.tile([P, C], F32, name="gated%d" % t) for t in range(PACK)]
+        hid = sb.tile([P, PACK, O], F32, name="hid")
+
+        def place_on_vector(window, offsets, staged, bank):
+            nc.vector.tensor_copy(staged, bank)
+            nc.vector.tensor_copy(window.indirect(offsets), staged)
+
+        def place_on_scalar(window, offsets, staged, bank):
+            nc.scalar.activation(out=staged, in_=bank, func=ACT.Copy)
+            nc.scalar.activation(out=window.indirect(offsets), in_=staged, func=ACT.Copy)
+
+        def apply_gate(t):
+            nc.vector.tensor_tensor(gated[t][:], board[t][:], gate[t][:], MULT)
+
+        place_on_vector(board[0][:], idx3[:], a_sb[0][:], a_ps[0][:])
+        place_on_scalar(board[2][:], idx3[:], a_sb[2][:], a_ps[2][:])
+        place_on_vector(board[1][:], idx3[:], a_sb[1][:], a_ps[1][:])
+        place_on_scalar(board[3][:], idx3[:], a_sb[3][:], a_ps[3][:])
+        apply_gate(0)
+        apply_gate(1)
+        nc.vector.tensor_copy(hid[:, 0, :], gated[0][:].indirect(idx5[:]))
+        apply_gate(2)
+        nc.vector.tensor_copy(hid[:, 1, :], gated[1][:].indirect(idx5[:]))
+        apply_gate(3)
+        nc.scalar.activation(out=hid[:, 2, :], in_=gated[2][:].indirect(idx5[:]), func=ACT.Copy)
+        nc.vector.tensor_copy(hid[:, 3, :], gated[3][:].indirect(idx5[:]))
+
+        hid_bf = sb.tile([P, O * PACK], BF16, name="hid_bf", align_bytes=64)
+        nc.vector.tensor_copy(
+            out=hid_bf[:].rearrange("p (c i t) -> p c t i", t=PACK, i=4),
+            in_=hid[:].rearrange("p t (c i) -> p c t i", i=4),
+        )
+        hid_w = sb.tile([P, O], U32, name="hid_w", align_bytes=64)
+        hid_s = sb.tile([P, O], U8, name="hid_s", align_bytes=64)
+        nc.vector.quantize_mx(out=hid_w[:].bitcast(E4M3X4), scales=hid_s[:], in_=hid_bf[:])
+
+        p_ps = [psum.tile([P, O], F32, name="p_ps%d" % h) for h in range(N // P)]
+        p_sb = [sb.tile([P, O], F32, name="p_sb%d" % h) for h in range(N // P)]
+        for h in range(N // P):
+            cols = slice(P * h, P * (h + 1))
+            nc.tensor.matmul_mx(
+                out=p_ps[h][:], lhsT=wb_w[:, cols].bitcast(E5M2X4), lhsT_scale=wb_s[:, cols],
+                rhs=hid_w[:].bitcast(E4M3X4), rhs_scale=hid_s[:], start=True, stop=True,
+            )
+        place_on_scalar(page[0][:], idx6[:], p_sb[0][:], p_ps[0][:])
+        place_on_vector(page[1][:], idx6[:], p_sb[1][:], p_ps[1][:])
+        nc.scalar.dma_start(out=out[0:P, :], in_=page[0][:])
+        nc.sync.dma_start(out=out[P : 2 * P, :], in_=page[1][:])

@@ -63,9 +63,8 @@ def tile_list_gatedpage_bank_one_scattered_kernel(
         w_s, w0_s, wb_s = weight_s[:, 0:R], weight_s[:, R : 2 * R], weight_s[:, 2 * R :]
         slope = sb.tile([P, PACK], F32, name="slope")
         offset = sb.tile([P, PACK], F32, name="offset")
-        gates = [sb.tile([P, Q], F32, name="gates%d" % t) for t in range(PACK)]
+        gates = [sb.tile([P, Q], F32, name="gates%d" % t, tag="wide%d" % t) for t in range(PACK)]
         board = [sb.tile([P, C], F32, name="board%d" % t) for t in range(PACK)]
-        page = [sb.tile([P, E], F32, name="page%d" % h) for h in range(N // P)]
 
         nc.vector.memset(xt_s[:].bitcast(I32), 0)
         nc.vector.memset(xo_s[:].bitcast(I32), 0)
@@ -74,30 +73,26 @@ def tile_list_gatedpage_bank_one_scattered_kernel(
             nc.vector.memset(board[t][:], 0.0)
 
         tg_rows = tg.rearrange("(p t) q -> p t q", t=PACK)
+        nc.gpsimd.dma_start(out=slope[:], in_=sg.rearrange("(p t) o -> p (t o)", t=PACK))
+        nc.gpsimd.dma_start(out=offset[:], in_=bg.rearrange("(p t) o -> p (t o)", t=PACK))
+        for t in range(PACK):
+            nc.gpsimd.dma_start(out=gates[t][:], in_=tg_rows[:, t, :])
         nc.sync.dma_start(idx[:], offs)
+        load_scale_rows(nc.sync, xt_s, xt_scales)
         nc.sync.dma_start(idx2[:], offs2)
-        nc.sync.dma_start(out=xt_w[:].bitcast(I32), in_=xt_words[0].rearrange("p n t -> p (n t)").bitcast(I32))
-        load_scale_rows(nc.scalar, xt_s, xt_scales)
         nc.sync.dma_start(out=xo_w[:].bitcast(I32), in_=xo_words[0].bitcast(I32))
-        load_scale_rows(nc.scalar, xo_s, xo_scales)
+        nc.sync.dma_start(out=xt_w[:].bitcast(I32), in_=xt_words[0].rearrange("p n t -> p (n t)").bitcast(I32))
+        nc.sync.dma_start(idx4[:], offs4)
+        load_scale_rows(nc.sync, xo_s, xo_scales)
         nc.sync.dma_start(out=w_w[:].bitcast(I32), in_=w_words[0].bitcast(I32))
         nc.sync.dma_start(out=w0_w[:], in_=w0_words[0].rearrange("p n t -> p (n t)").bitcast(I32))
         load_scale_rows(nc.sync, w_s, w_scales)
         load_scale_rows(nc.sync, w0_s, w0_scales)
-        nc.sync.dma_start(out=gates[0][:], in_=tg_rows[:, 0, :])
-        nc.sync.dma_start(idx4[:], offs4)
-        nc.sync.dma_start(out=slope[:], in_=sg.rearrange("(p t) o -> p (t o)", t=PACK))
-        nc.sync.dma_start(out=offset[:], in_=bg.rearrange("(p t) o -> p (t o)", t=PACK))
-        nc.sync.dma_start(out=gates[1][:], in_=tg_rows[:, 1, :])
         nc.sync.dma_start(idx3[:], offs3)
-        nc.sync.dma_start(out=gates[2][:], in_=tg_rows[:, 2, :])
-        nc.sync.dma_start(out=gates[3][:], in_=tg_rows[:, 3, :])
         nc.sync.dma_start(idx5[:], offs5)
         nc.sync.dma_start(idx6[:], offs6)
         nc.sync.dma_start(out=wb_w[:], in_=wb_words[0].rearrange("p n t -> p (n t)").bitcast(I32))
         load_scale_rows(nc.sync, wb_s, wb_scales)
-        for h in range(N // P):
-            nc.vector.memset(page[h][:], 0.0)
 
         tok_w = sb.tile([P, J], U32, name="tok_w", align_bytes=64)
         tok_s = sb.tile([P, J], U8, name="tok_s", align_bytes=64)
@@ -107,12 +102,12 @@ def tile_list_gatedpage_bank_one_scattered_kernel(
         w0_wd = sb.tile([P, R], I32, name="w0_wd", align_bytes=64)
         w_sd = sb.tile([P, R], U8, name="w_sd", align_bytes=64)
         w0_sd = sb.tile([P, R], U8, name="w0_sd", align_bytes=64)
-        nc.vector.tensor_copy(tok_w[:], xt_w[:].indirect(idx[:]))
-        nc.vector.tensor_copy(note_w[:], xo_w[:].indirect(idx2[:]))
         nc.vector.tensor_copy(tok_s[:], xt_s[:].indirect(idx[:]))
+        nc.vector.tensor_copy(note_w[:], xo_w[:].indirect(idx2[:]))
+        nc.vector.tensor_copy(tok_w[:], xt_w[:].indirect(idx[:]))
+        nc.vector.tensor_copy(note_s[:], xo_s[:].indirect(idx2[:]))
         deal_columns(nc, w_wd[:], w_w[:], 8)
         deal_columns(nc, w0_wd[:], w0_w[:], 4)
-        nc.vector.tensor_copy(note_s[:], xo_s[:].indirect(idx2[:]))
         deal_columns(nc, w_sd[:], w_s, 16)
         deal_columns(nc, w0_sd[:], w0_s, 16)
 
@@ -123,8 +118,12 @@ def tile_list_gatedpage_bank_one_scattered_kernel(
                 bias=offset[:, t : t + 1], scale=slope[:, t : t + 1],
             )
 
+        page = [sb.tile([P, E], F32, name="page%d" % h, tag="wide%d" % (h + 2)) for h in range(N // P)]
+        for h in range(N // P):
+            nc.gpsimd.memset(page[h][:], 0.0)
+
         a_ps = [psum.tile([P, J], F32, name="a_ps%d" % t) for t in range(PACK)]
-        for t in (0, 2, 1, 3):
+        for t in range(PACK):
             cols = slice(P * t, P * (t + 1))
             nc.tensor.matmul_mx(
                 out=a_ps[t][:], lhsT=w_wd[:, cols].bitcast(E2M1X4), lhsT_scale=w_sd[:, cols],
@@ -154,33 +153,37 @@ def tile_list_gatedpage_bank_one_scattered_kernel(
         place_on_scalar(board[2][:], idx3[:], a_sb[2][:], a_ps[2][:])
         place_on_vector(board[1][:], idx3[:], a_sb[1][:], a_ps[1][:])
         place_on_scalar(board[3][:], idx3[:], a_sb[3][:], a_ps[3][:])
-        apply_gate(0)
-        apply_gate(1)
-        nc.vector.tensor_copy(hid[:, 0, :], gated[0][:].indirect(idx5[:]))
-        apply_gate(2)
-        nc.vector.tensor_copy(hid[:, 1, :], gated[1][:].indirect(idx5[:]))
-        apply_gate(3)
-        nc.scalar.activation(out=hid[:, 2, :], in_=gated[2][:].indirect(idx5[:]), func=ACT.Copy)
-        nc.vector.tensor_copy(hid[:, 3, :], gated[3][:].indirect(idx5[:]))
+        for t in range(PACK):
+            apply_gate(t)
+        half = O // 2
+        reads = [slice(u * half, (u + 1) * half) for u in range(2)]
+        entries = [slice(u * half // 16, (u + 1) * half // 16) for u in range(2)]
+        for t in (0, 1):
+            nc.scalar.activation(out=hid[:, t, :], in_=gated[t][:].indirect(idx5[:]), func=ACT.Copy)
+        for u in range(2):
+            nc.scalar.activation(out=hid[:, 2, reads[u]], in_=gated[2][:].indirect(idx5[:, entries[u]]), func=ACT.Copy)
+            nc.vector.tensor_copy(hid[:, 3, reads[u]], gated[3][:].indirect(idx5[:, entries[u]]))
 
-        hid_bf = sb.tile([P, O * PACK], BF16, name="hid_bf", align_bytes=64)
-        nc.vector.tensor_copy(
-            out=hid_bf[:].rearrange("p (c i t) -> p c t i", t=PACK, i=4),
-            in_=hid[:].rearrange("p t (c i) -> p c t i", i=4),
-        )
-        hid_w = sb.tile([P, O], U32, name="hid_w", align_bytes=64)
-        hid_s = sb.tile([P, O], U8, name="hid_s", align_bytes=64)
-        nc.vector.quantize_mx(out=hid_w[:].bitcast(E4M3X4), scales=hid_s[:], in_=hid_bf[:])
-
-        p_ps = [psum.tile([P, O], F32, name="p_ps%d" % h) for h in range(N // P)]
-        p_sb = [sb.tile([P, O], F32, name="p_sb%d" % h) for h in range(N // P)]
-        for h in range(N // P):
-            cols = slice(P * h, P * (h + 1))
-            nc.tensor.matmul_mx(
-                out=p_ps[h][:], lhsT=wb_w[:, cols].bitcast(E5M2X4), lhsT_scale=wb_s[:, cols],
-                rhs=hid_w[:].bitcast(E4M3X4), rhs_scale=hid_s[:], start=True, stop=True,
+        hid_bf = [sb.tile([P, half * PACK], BF16, name="hid_bf%d" % u, align_bytes=64) for u in range(2)]
+        hid_w = [sb.tile([P, half], U32, name="hid_w%d" % u, align_bytes=64) for u in range(2)]
+        hid_s = [sb.tile([P, half], U8, name="hid_s%d" % u, align_bytes=64) for u in range(2)]
+        for u, copy in enumerate((nc.vector.tensor_copy, nc.scalar.copy)):
+            copy(
+                out=hid_bf[u][:].rearrange("p (c i t) -> p c t i", t=PACK, i=4),
+                in_=hid[:, :, reads[u]].rearrange("p t (c i) -> p c t i", i=4),
             )
-        place_on_scalar(page[0][:], idx6[:], p_sb[0][:], p_ps[0][:])
-        place_on_vector(page[1][:], idx6[:], p_sb[1][:], p_ps[1][:])
+        for u in range(2):
+            nc.vector.quantize_mx(out=hid_w[u][:].bitcast(E4M3X4), scales=hid_s[u][:], in_=hid_bf[u][:])
+
+        p_sb = [sb.tile([P, O], F32, name="p_sb%d" % h) for h in range(N // P)]
+        for u in range(2):
+            for h, place in enumerate((place_on_scalar, place_on_vector)):
+                cols = slice(P * h, P * (h + 1))
+                p_ps = psum.tile([P, half], F32, name="p_ps%d%d" % (u, h))
+                nc.tensor.matmul_mx(
+                    out=p_ps[:], lhsT=wb_w[:, cols].bitcast(E5M2X4), lhsT_scale=wb_s[:, cols],
+                    rhs=hid_w[u][:].bitcast(E4M3X4), rhs_scale=hid_s[u][:], start=True, stop=True,
+                )
+                place(page[h][:], idx6[:, entries[u]], p_sb[h][:, reads[u]], p_ps[:])
         nc.scalar.dma_start(out=out[0:P, :], in_=page[0][:])
         nc.sync.dma_start(out=out[P : 2 * P, :], in_=page[1][:])

@@ -52,25 +52,29 @@ def tile_list_gatedpage_bank_one_scattered_kernel(
         idx5 = lists.tile([P, O // 16], U16, name="idx5")
         idx6 = lists.tile([P, O // 16], U16, name="idx6")
 
-        xt_w = sb.tile([P, T], U32, name="xt_w", align_bytes=64)
+        xt_w = sb.tile([P, T], U32, name="xt_w", tag="reuse0", align_bytes=64)
         xt_s = sb.tile([P, T], U8, name="xt_s", align_bytes=64)
         xo_w = sb.tile([P, Z], U16, name="xo_w", align_bytes=64)
         xo_s = sb.tile([P, Z], U8, name="xo_s", align_bytes=64)
         w_w = sb.tile([P, R], U16, name="w_w", align_bytes=64)
-        w0_w = sb.tile([P, R], I32, name="w0_w", align_bytes=64)
+        w0_w = sb.tile([P, R], I32, name="w0_w", tag="reuse1", align_bytes=64)
         wb_w = sb.tile([P, N], I32, name="wb_w", align_bytes=64)
         weight_s = sb.tile([P, R + R + N], U8, name="weight_s", align_bytes=64)
         w_s, w0_s, wb_s = weight_s[:, 0:R], weight_s[:, R : 2 * R], weight_s[:, 2 * R :]
         slope = sb.tile([P, PACK], F32, name="slope")
         offset = sb.tile([P, PACK], F32, name="offset")
-        gates = [sb.tile([P, Q], F32, name="gates%d" % t, tag="wide%d" % t) for t in range(PACK)]
+        gates = [sb.tile([P, Q], F32, name="gates%d" % t) for t in range(PACK)]
         board = [sb.tile([P, C], F32, name="board%d" % t) for t in range(PACK)]
 
         nc.vector.memset(xt_s[:].bitcast(I32), 0)
+        warm_in = sb.tile([P, 1], F32, name="warm_in")
+        warm_out = sb.tile([P, 1], F32, name="warm_out")
+        nc.vector.memset(warm_in[:], 0.0)
+        nc.scalar.activation(out=warm_out[:], in_=warm_in[:], func=ACT.Sigmoid)
         nc.vector.memset(xo_s[:].bitcast(I32), 0)
         nc.vector.memset(weight_s[:].bitcast(I32), 0)
         for t in range(PACK):
-            nc.vector.memset(board[t][:], 0.0)
+            nc.vector.memset(board[t][:].bitcast(I32), 0)
 
         tg_rows = tg.rearrange("(p t) q -> p t q", t=PACK)
         nc.gpsimd.dma_start(out=slope[:], in_=sg.rearrange("(p t) o -> p (t o)", t=PACK))
@@ -111,6 +115,10 @@ def tile_list_gatedpage_bank_one_scattered_kernel(
         deal_columns(nc, w_sd[:], w_s, 16)
         deal_columns(nc, w0_sd[:], w0_s, 16)
 
+        page = [sb.tile([P, E], F32, name="page%d" % h, tag="reuse%d" % h, align_bytes=64) for h in range(N // P)]
+        for h in range(N // P):
+            nc.vector.memset(page[h][:].bitcast(I32), 0)
+
         gate = [sb.tile([P, C], F32, name="gate%d" % t) for t in range(PACK)]
         for t in range(PACK):
             nc.scalar.activation(
@@ -118,20 +126,16 @@ def tile_list_gatedpage_bank_one_scattered_kernel(
                 bias=offset[:, t : t + 1], scale=slope[:, t : t + 1],
             )
 
-        page = [sb.tile([P, E], F32, name="page%d" % h, tag="wide%d" % (h + 2)) for h in range(N // P)]
-        for h in range(N // P):
-            nc.gpsimd.memset(page[h][:], 0.0)
-
         a_ps = [psum.tile([P, J], F32, name="a_ps%d" % t) for t in range(PACK)]
         for t in range(PACK):
             cols = slice(P * t, P * (t + 1))
             nc.tensor.matmul_mx(
-                out=a_ps[t][:], lhsT=w_wd[:, cols].bitcast(E2M1X4), lhsT_scale=w_sd[:, cols],
-                rhs=tok_w[:].bitcast(E4M3X4), rhs_scale=tok_s[:], start=True, stop=False,
+                out=a_ps[t][:], lhsT=w0_wd[:, cols].bitcast(E5M2X4), lhsT_scale=w0_sd[:, cols],
+                rhs=note_w[:].bitcast(E2M1X4), rhs_scale=note_s[:], start=True, stop=False,
             )
             nc.tensor.matmul_mx(
-                out=a_ps[t][:], lhsT=w0_wd[:, cols].bitcast(E5M2X4), lhsT_scale=w0_sd[:, cols],
-                rhs=note_w[:].bitcast(E2M1X4), rhs_scale=note_s[:], start=False, stop=True,
+                out=a_ps[t][:], lhsT=w_wd[:, cols].bitcast(E2M1X4), lhsT_scale=w_sd[:, cols],
+                rhs=tok_w[:].bitcast(E4M3X4), rhs_scale=tok_s[:], start=False, stop=True,
             )
 
         a_sb = [sb.tile([P, J], F32, name="a_sb%d" % t) for t in range(PACK)]

from contextlib import ExitStack

import concourse.mybir as mybir

F32 = mybir.dt.float32
BF16 = mybir.dt.bfloat16
I32 = mybir.dt.int32
U32 = mybir.dt.uint32
U16 = mybir.dt.uint16
U8 = mybir.dt.uint8
E4M3X4 = mybir.dt.float8_e4m3fn_x4
E5M2X4 = mybir.dt.float8_e5m2_x4
E2M1X4 = mybir.dt.float4_e2m1fn_x4
ACT = mybir.ActivationFunctionType
MULT = mybir.AluOpType.mult

P = 128
PACK = 4
T, Z, J, R, C, Q, O, N, E = 1024, 1024, 256, 512, 512, 1024, 256, 256, 1024
FLOPS = 2 * 512 * R * J * 2 + 2 * R * N * O


def load_scale_rows(queue, plane, scales):
    for quad in range(4):
        queue.dma_start(
            out=plane[32 * quad : 32 * quad + 4, :].bitcast(I32),
            in_=scales[0, 4 * quad : 4 * quad + 4, :].bitcast(I32),
        )


def deal_columns(nc, dealt, natural, run):
    nc.vector.tensor_copy(
        out=dealt.rearrange("p (t c i) -> p c t i", t=PACK, i=run),
        in_=natural.rearrange("p (c i t) -> p c t i", t=PACK, i=run),
    )


def tile_list_gatedpage_bank_one_scattered_kernel(
    tc, xt_words, xt_scales, w_words, w_scales, xo_words, xo_scales, w0_words, w0_scales,
    tg, sg, bg, wb_words, wb_scales, offs, offs2, offs3, offs4, offs5, offs6, out,
):
    nc = tc.nc
    with ExitStack() as ctx:
        lists = ctx.enter_context(tc.tile_pool(name="lists", bufs=1))
        sb = ctx.enter_context(tc.tile_pool(name="sb", bufs=1))
        psum = ctx.enter_context(tc.psum_pool(name="psum", bufs=1))

        idx = lists.tile([P, J // 16], U16, name="idx")
        idx2 = lists.tile([P, J // 16], U16, name="idx2")
        idx3 = lists.tile([P, J // 16], U16, name="idx3")
        idx4 = lists.tile([P, C // 16], U16, name="idx4")
        idx5 = lists.tile([P, O // 16], U16, name="idx5")
        idx6 = lists.tile([P, O // 16], U16, name="idx6")

        xt_w = sb.tile([P, T], U32, name="xt_w", tag="reuse0", align_bytes=64)
        xt_s = sb.tile([P, T], U8, name="xt_s", align_bytes=64)
        xo_w = sb.tile([P, Z], U16, name="xo_w", align_bytes=64)
        xo_s = sb.tile([P, Z], U8, name="xo_s", align_bytes=64)
        w_w = sb.tile([P, R], U16, name="w_w", align_bytes=64)
        w0_w = sb.tile([P, R], I32, name="w0_w", tag="reuse1", align_bytes=64)
        wb_w = sb.tile([P, N], I32, name="wb_w", align_bytes=64)
        weight_s = sb.tile([P, R + R + N], U8, name="weight_s", align_bytes=64)
        w_s, w0_s, wb_s = weight_s[:, 0:R], weight_s[:, R : 2 * R], weight_s[:, 2 * R :]
        slope = sb.tile([P, PACK], F32, name="slope")
        offset = sb.tile([P, PACK], F32, name="offset")
        gates = [sb.tile([P, Q], F32, name="gates%d" % t) for t in range(PACK)]
        board = [sb.tile([P, C], F32, name="board%d" % t) for t in range(PACK)]

        nc.vector.memset(xt_s[:].bitcast(I32), 0)
        warm_in = sb.tile([P, 1], F32, name="warm_in")
        warm_out = sb.tile([P, 1], F32, name="warm_out")
        nc.vector.memset(warm_in[:], 0.0)
        nc.scalar.activation(out=warm_out[:], in_=warm_in[:], func=ACT.Sigmoid)
        nc.vector.memset(xo_s[:].bitcast(I32), 0)
        nc.vector.memset(weight_s[:].bitcast(I32), 0)
        for t in range(PACK):
            nc.vector.memset(board[t][:].bitcast(I32), 0)

        tg_rows = tg.rearrange("(p t) q -> p t q", t=PACK)
        nc.gpsimd.dma_start(out=slope[:], in_=sg.rearrange("(p t) o -> p (t o)", t=PACK))
        nc.gpsimd.dma_start(out=offset[:], in_=bg.rearrange("(p t) o -> p (t o)", t=PACK))
        for t in range(PACK):
            nc.gpsimd.dma_start(out=gates[t][:], in_=tg_rows[:, t, :])
        nc.sync.dma_start(idx[:], offs)
        load_scale_rows(nc.sync, xt_s, xt_scales)
        nc.sync.dma_start(idx2[:], offs2)
        nc.sync.dma_start(out=xo_w[:].bitcast(I32), in_=xo_words[0].bitcast(I32))
        nc.sync.dma_start(out=xt_w[:].bitcast(I32), in_=xt_words[0].rearrange("p n t -> p (n t)").bitcast(I32))
        nc.sync.dma_start(idx4[:], offs4)
        load_scale_rows(nc.sync, xo_s, xo_scales)
        nc.sync.dma_start(out=w_w[:].bitcast(I32), in_=w_words[0].bitcast(I32))
        nc.sync.dma_start(out=w0_w[:], in_=w0_words[0].rearrange("p n t -> p (n t)").bitcast(I32))
        load_scale_rows(nc.sync, w_s, w_scales)
        load_scale_rows(nc.sync, w0_s, w0_scales)
        nc.sync.dma_start(idx3[:], offs3)
        nc.sync.dma_start(idx5[:], offs5)
        nc.sync.dma_start(idx6[:], offs6)
        nc.sync.dma_start(out=wb_w[:], in_=wb_words[0].rearrange("p n t -> p (n t)").bitcast(I32))
        load_scale_rows(nc.sync, wb_s, wb_scales)

        tok_w = sb.tile([P, J], U32, name="tok_w", align_bytes=64)
        tok_s = sb.tile([P, J], U8, name="tok_s", align_bytes=64)
        note_w = sb.tile([P, J], U16, name="note_w", align_bytes=64)
        note_s = sb.tile([P, J], U8, name="note_s", align_bytes=64)
        w_wd = sb.tile([P, R], U16, name="w_wd", align_bytes=64)
        w0_wd = sb.tile([P, R], I32, name="w0_wd", align_bytes=64)
        w_sd = sb.tile([P, R], U8, name="w_sd", align_bytes=64)
        w0_sd = sb.tile([P, R], U8, name="w0_sd", align_bytes=64)
        nc.vector.tensor_copy(tok_s[:], xt_s[:].indirect(idx[:]))
        nc.vector.tensor_copy(note_w[:], xo_w[:].indirect(idx2[:]))
        nc.vector.tensor_copy(tok_w[:], xt_w[:].indirect(idx[:]))
        nc.vector.tensor_copy(note_s[:], xo_s[:].indirect(idx2[:]))
        deal_columns(nc, w_wd[:], w_w[:], 8)
        deal_columns(nc, w0_wd[:], w0_w[:], 4)
        deal_columns(nc, w_sd[:], w_s, 16)
        deal_columns(nc, w0_sd[:], w0_s, 16)

        page = [sb.tile([P, E], F32, name="page%d" % h, tag="reuse%d" % h, align_bytes=64) for h in range(N // P)]
        for h in range(N // P):
            nc.vector.memset(page[h][:].bitcast(I32), 0)

        gate = [sb.tile([P, C], F32, name="gate%d" % t) for t in range(PACK)]
        for t in range(PACK):
            nc.scalar.activation(
                out=gate[t][:], in_=gates[t][:].indirect(idx4[:]), func=ACT.Sigmoid,
                bias=offset[:, t : t + 1], scale=slope[:, t : t + 1],
            )

        a_ps = [psum.tile([P, J], F32, name="a_ps%d" % t) for t in range(PACK)]
        for t in range(PACK):
            cols = slice(P * t, P * (t + 1))
            nc.tensor.matmul_mx(
                out=a_ps[t][:], lhsT=w0_wd[:, cols].bitcast(E5M2X4), lhsT_scale=w0_sd[:, cols],
                rhs=note_w[:].bitcast(E2M1X4), rhs_scale=note_s[:], start=True, stop=False,
            )
            nc.tensor.matmul_mx(
                out=a_ps[t][:], lhsT=w_wd[:, cols].bitcast(E2M1X4), lhsT_scale=w_sd[:, cols],
                rhs=tok_w[:].bitcast(E4M3X4), rhs_scale=tok_s[:], start=False, stop=True,
            )

        a_sb = [sb.tile([P, J], F32, name="a_sb%d" % t) for t in range(PACK)]
        gated = [sb.tile([P, C], F32, name="gated%d" % t) for t in range(PACK)]
        hid = sb.tile([P, PACK, O], F32, name="hid")

        def place_on_vector(window, offsets, staged, bank):
            nc.vector.tensor_copy(staged, bank)
            nc.vector.tensor_copy(window.indirect(offsets), staged)

        def place_on_scalar(window, offsets, staged, bank):
            nc.scalar.activation(out=staged, in_=bank, func=ACT.Copy)
            nc.scalar.activation(out=window.indirect(offsets), in_=staged, func=ACT.Copy)

        def apply_gate(t):
            nc.vector.tensor_tensor(gated[t][:], board[t][:], gate[t][:], MULT)

        place_on_vector(board[0][:], idx3[:], a_sb[0][:], a_ps[0][:])
        place_on_scalar(board[2][:], idx3[:], a_sb[2][:], a_ps[2][:])
        place_on_vector(board[1][:], idx3[:], a_sb[1][:], a_ps[1][:])
        place_on_scalar(board[3][:], idx3[:], a_sb[3][:], a_ps[3][:])
        for t in range(PACK):
            apply_gate(t)
        half = O // 2
        reads = [slice(u * half, (u + 1) * half) for u in range(2)]
        entries = [slice(u * half // 16, (u + 1) * half // 16) for u in range(2)]
        for t in (0, 1):
            nc.scalar.activation(out=hid[:, t, :], in_=gated[t][:].indirect(idx5[:]), func=ACT.Copy)
        for u in range(2):
            nc.scalar.activation(out=hid[:, 2, reads[u]], in_=gated[2][:].indirect(idx5[:, entries[u]]), func=ACT.Copy)
            nc.vector.tensor_copy(hid[:, 3, reads[u]], gated[3][:].indirect(idx5[:, entries[u]]))

        hid_bf = [sb.tile([P, half * PACK], BF16, name="hid_bf%d" % u, align_bytes=64) for u in range(2)]
        hid_w = [sb.tile([P, half], U32, name="hid_w%d" % u, align_bytes=64) for u in range(2)]
        hid_s = [sb.tile([P, half], U8, name="hid_s%d" % u, align_bytes=64) for u in range(2)]
        for u, copy in enumerate((nc.vector.tensor_copy, nc.scalar.copy)):
            copy(
                out=hid_bf[u][:].rearrange("p (c i t) -> p c t i", t=PACK, i=4),
                in_=hid[:, :, reads[u]].rearrange("p t (c i) -> p c t i", i=4),
            )
        for u in range(2):
            nc.vector.quantize_mx(out=hid_w[u][:].bitcast(E4M3X4), scales=hid_s[u][:], in_=hid_bf[u][:])

        p_sb = [sb.tile([P, O], F32, name="p_sb%d" % h) for h in range(N // P)]
        for u in range(2):
            for h, place in enumerate((place_on_scalar, place_on_vector)):
                cols = slice(P * h, P * (h + 1))
                p_ps = psum.tile([P, half], F32, name="p_ps%d%d" % (u, h))
                nc.tensor.matmul_mx(
                    out=p_ps[:], lhsT=wb_w[:, cols].bitcast(E5M2X4), lhsT_scale=wb_s[:, cols],
                    rhs=hid_w[u][:].bitcast(E4M3X4), rhs_scale=hid_s[u][:], start=True, stop=True,
                )
                place(page[h][:], idx6[:, entries[u]], p_sb[h][:, reads[u]], p_ps[:])
        nc.scalar.dma_start(out=out[0:P, :], in_=page[0][:])
        nc.sync.dma_start(out=out[P : 2 * P, :], in_=page[1][:])
